import numpy as np
import ml_dtypes


def mxq(x, axis, fmt="e4m3"):
    dtype, down = {"e4m3": (ml_dtypes.float8_e4m3fn, 7), "e5m2": (ml_dtypes.float8_e5m2, 14)}[fmt]
    v = np.moveaxis(np.asarray(x, np.float32).astype(ml_dtypes.bfloat16).astype(np.float64), axis, -1)
    blocks = v.reshape(v.shape[:-1] + (-1, 32))
    amax = np.abs(blocks).max(-1, keepdims=True)
    byte = np.maximum(np.where(amax > 0, np.frexp(amax)[1] - 1 + 127, 0) - down, 1)
    scale = np.exp2(byte - 127.0)
    codes = (blocks / scale).astype(np.float32).astype(dtype).astype(np.float64)
    return np.moveaxis((codes * scale).reshape(v.shape), -1, axis)


WIDE = False


def mx_kscale(k):
    if not WIDE:
        return np.ones(k)
    levels = np.array([10, -10, 5, -5, 0])
    if k % 512:
        return np.exp2(np.random.permutation(np.resize(levels, k // 32))).repeat(32)
    a = np.empty((k // 512, 16))
    for p in range(k // 512):
        a[p, :8] = np.random.permutation(np.resize(levels, 8))
        for g in range(8):
            far = levels[np.abs(levels - a[p, g]) >= 10]
            a[p, g + 8] = far[np.random.randint(len(far))]
    return np.exp2(a.ravel()).repeat(32)


BF16 = ml_dtypes.bfloat16


def bf(x):
    return np.asarray(x, np.float32).astype(BF16)


def f64(x):
    return np.asarray(x).astype(np.float64)


B, N1, K1, N2, K2 = 2, 512, 512, 512, 512


def left_transform(fq, xq):
    return fq @ xq


def twiddle(ar, ai, tr, ti):
    pr = ar * tr[None, :, :] - ai * ti[None, :, :]
    pi = ar * ti[None, :, :] + ai * tr[None, :, :]
    return pr, pi


def draw0():
    s, t = mx_kscale(N1), mx_kscale(N2)
    s1 = 1.0 / np.sqrt(N1)
    s2 = 1.0 / np.sqrt(N2)
    return {
        "x": bf(np.random.standard_normal((B, N1, N2)) * s[None, :, None]),
        "f1r": bf(np.random.standard_normal((K1, N1)) * s1 / s[None, :]),
        "f1i": bf(np.random.standard_normal((K1, N1)) * s1 / s[None, :]),
        "tr": bf(np.random.standard_normal((K1, N2)) * 0.7 * t[None, :]),
        "ti": bf(np.random.standard_normal((K1, N2)) * 0.7 * t[None, :]),
        "f2r": bf(np.random.standard_normal((N2, K2)) * s2 / t[:, None]),
        "f2i": bf(np.random.standard_normal((N2, K2)) * s2 / t[:, None]),
    }


def core(x, f1r, f1i, tr, ti, f2r, f2i):
    xq = mxq(f64(x), 1, "e4m3")
    ar = left_transform(mxq(f64(f1r), 1, "e4m3"), xq)
    ai = left_transform(mxq(f64(f1i), 1, "e4m3"), xq)
    pr, pi = twiddle(ar, ai, f64(tr), f64(ti))
    yr = mxq(pr, 2, "e4m3") @ mxq(f64(f2r), 0, "e4m3")
    yi = mxq(pi, 2, "e4m3") @ mxq(f64(f2i), 0, "e4m3")
    return yr - yi


def e4m3fn_bytes(y):
    return np.clip(np.asarray(y, np.float64), -448.0, 448.0).astype(np.float32).astype(ml_dtypes.float8_e4m3fn).view(np.uint8)


def e4m3fn_values(b):
    return np.asarray(b, np.uint8).view(ml_dtypes.float8_e4m3fn).astype(np.float64)


def setup_inputs():
    d = draw0()
    x0 = np.asarray(d['x']).astype(np.float64)
    s = (np.max(np.abs(x0), axis=(0, 2), keepdims=True) / 448.0).astype(np.float32)
    out = {}
    for k, v in d.items():
        if k == 'x':
            out['x_bytes'] = e4m3fn_bytes(x0 / s.astype(np.float64))
            out['x_scale'] = s
        else:
            out[k] = v
    return out


def reference(x_bytes, x_scale, f1r, f1i, tr, ti, f2r, f2i):
    return core(e4m3fn_values(x_bytes) * x_scale.astype(np.float64), f1r, f1i, tr, ti, f2r, f2i)

@@ -1,0 +1,367 @@
+from contextlib import ExitStack
+
+import concourse.mybir as mybir
+from concourse.masks import make_identity
+
+F32 = mybir.dt.float32
+BF16 = mybir.dt.bfloat16
+U32 = mybir.dt.uint32
+U8 = mybir.dt.uint8
+FP8 = mybir.dt.float8_e4m3fn
+FP8X4 = mybir.dt.float8_e4m3fn_x4
+MULT = mybir.AluOpType.mult
+ADD = mybir.AluOpType.add
+COPY = mybir.ActivationFunctionType.Copy
+
+P = 128
+PACK = 4
+N = 512
+B = 2
+KT = 4
+STEPS = B * KT
+FLOPS = 2 * 4 * 2 * 512 * 512 * 512
+
+
+def tile_learnedfoursteptwiddletransform_kernel(tc, x_bytes, x_scale, f1r, f1i, tr, ti, f2r, f2i, out):
+    nc = tc.nc
+    with ExitStack() as ctx:
+        keep = ctx.enter_context(tc.tile_pool(name="keep", bufs=1))
+        work = ctx.enter_context(tc.tile_pool(name="work", bufs=2))
+        psum = ctx.enter_context(tc.psum_pool(name="psum", bufs=1))
+        ctx.enter_context(tc.manual_schedule())
+
+        def by_tile(mat):
+            return mat.rearrange("(p a) j -> p a j", a=KT)
+
+        xs = keep.tile([P, PACK], F32, name="xs")
+        xb = [keep.tile([P, PACK * N], U8, name="xbytes%d" % b) for b in range(B)]
+        f1_groups = [(0, 1), (1, 3), (3, 4)]
+        t_groups = [(0, 1), (1, 2), (2, 4)]
+        f1_raw = {}
+        tw = {}
+        f2_raw = [keep.tile([P, PACK, N], BF16, name="f2raw%d" % c) for c in range(2)]
+
+        def load_x(b):
+            nc.sync.dma_start(out=xb[b][:], in_=x_bytes[b].rearrange("(p t) n -> p (t n)", t=PACK))
+
+        def load_f1(g):
+            lo, hi = f1_groups[g]
+            for c, mat in enumerate((f1r, f1i)):
+                raw = keep.tile([P, hi - lo, N], BF16, name="f1raw%d_%d" % (g, c))
+                nc.sync.dma_start(out=raw[:], in_=by_tile(mat)[:, lo:hi, :])
+                for kt in range(lo, hi):
+                    f1_raw[(kt, c)] = raw[:, kt - lo, :]
+
+        def load_t(g):
+            lo, hi = t_groups[g]
+            table = keep.tile([P, 3, hi - lo, N], BF16, name="tw%d" % g)
+            for slot, mat in ((1, tr), (2, ti)):
+                nc.sync.dma_start(out=table[:, slot, :, :], in_=by_tile(mat)[:, lo:hi, :])
+            tw[g] = table
+
+        def load_f2(c):
+            rows = (f2r, f2i)[c].rearrange("(g t r) m -> t g r m", t=PACK, r=8)
+            for t in range(PACK):
+                nc.sync.dma_start(out=f2_raw[c][:, t, :], in_=rows[t])
+
+        nc.sync.dma_start(out=xs[:], in_=x_scale.rearrange("o (p t) z -> p (o t z)", t=PACK))
+        load_x(0)
+        load_f1(0)
+        load_t(0)
+        load_f1(1)
+        load_x(1)
+        load_f2(0)
+        load_t(1)
+        load_f1(2)
+        load_t(2)
+        load_f2(1)
+
+        ident = keep.tile([P, P], F32, name="ident")
+        make_identity(nc, ident[:])
+
+        xw = [keep.tile([P, PACK, N], BF16, name="xw%d" % b) for b in range(B)]
+        xg = [keep.tile([P, N, PACK], BF16, name="xg%d" % b, align_bytes=64) for b in range(B)]
+        xq = [keep.tile([P, N], U32, name="xq%d" % b, align_bytes=64) for b in range(B)]
+        xsc = [keep.tile([P, N], U8, name="xsc%d" % b, align_bytes=64) for b in range(B)]
+        f1g = {}
+        f1q = [keep.tile([P, 2 * P], U32, name="f1q%d" % kt, align_bytes=64) for kt in range(KT)]
+        f1sc = [keep.tile([P, 2 * P], U8, name="f1sc%d" % kt, align_bytes=64) for kt in range(KT)]
+        f2q = [keep.tile([P, N], U32, name="f2q%d" % c, align_bytes=64) for c in range(2)]
+        f2sc = [keep.tile([P, N], U8, name="f2sc%d" % c, align_bytes=64) for c in range(2)]
+        pq = [keep.tile([P, 2 * P], U32, name="pq%d" % s, align_bytes=64) for s in range(STEPS)]
+        psc = [keep.tile([P, 2 * P], U8, name="psc%d" % s, align_bytes=64) for s in range(STEPS)]
+        a_banks = {}
+        prods = {}
+        p_banks = {}
+        pg = {}
+        f1_banks = {}
+        o_banks = {}
+        f2g = {}
+
+        def quantize(codes, scales, src):
+            nc.vector.quantize_mx(out=codes.bitcast(FP8X4), scales=scales, in_=src)
+
+        def widen_x(b, t, on_vector):
+            src = xb[b][:, t * N : (t + 1) * N].bitcast(FP8)
+            if on_vector:
+                nc.vector.tensor_scalar(out=xw[b][:, t, :], in0=src, scalar1=xs[:, t : t + 1], scalar2=None, op0=MULT)
+            else:
+                nc.scalar.activation(out=xw[b][:, t, :], in_=src, func=COPY, scale=xs[:, t : t + 1])
+
+        def interleave_x(b, lo, hi, on_vector):
+            dst = xg[b][:, lo:hi, :].rearrange("p (c i) t -> p c t i", i=4)
+            src = xw[b][:, :, lo:hi].rearrange("p t (c i) -> p c t i", i=4)
+            if on_vector:
+                nc.vector.tensor_copy(out=dst, in_=src)
+            else:
+                nc.scalar.copy(out=dst, in_=src)
+
+        def quantize_x(b):
+            quantize(xq[b][:], xsc[b][:], xg[b][:].rearrange("p n t -> p (n t)"))
+
+        def transpose_f1(kt):
+            bank = psum.tile([P, 2, 2, P], F32, name="f1bank", tag="o", bufs=2)
+            for c in range(2):
+                words = f1_raw[(kt, c)].bitcast(F32)
+                for u in range(2):
+                    nc.tensor.transpose(bank[:, c, u, :], words[:, u : 2 * P : 2], ident[:])
+            f1_banks[kt] = bank
+
+        def copy_f1(kt):
+            if kt == 1:
+                grouped = keep.tile([P, 2 * P * PACK], BF16, name="f1stage", tag="stage", align_bytes=64)
+            else:
+                grouped = keep.tile([P, 2 * P * PACK], BF16, name="f1g%d" % kt, align_bytes=64)
+            nc.scalar.copy(
+                out=grouped[:].bitcast(F32).rearrange("p (c k u) -> p c k u", c=2, u=2),
+                in_=f1_banks[kt][:].rearrange("p c u k -> p c k u"),
+            )
+            f1g[kt] = grouped
+
+        def quantize_f1(kt):
+            quantize(f1q[kt][:], f1sc[kt][:], f1g[kt][:])
+
+        def negate_ti(g):
+            nc.vector.tensor_scalar(
+                out=tw[g][:, 0, :, :], in0=tw[g][:, 2, :, :], scalar1=-1.0, scalar2=None, op0=MULT
+            )
+
+        def interleave_f2(ch):
+            c, half = divmod(ch, 2)
+            grouped = keep.tile([P, 2 * P * PACK], BF16, name="f2stage", tag="stage", align_bytes=64)
+            nc.gpsimd.tensor_scalar(
+                out=grouped[:].rearrange("p (m t) -> p m t", t=PACK),
+                in0=f2_raw[c][:, :, half * 256 : (half + 1) * 256].rearrange("p t m -> p m t"),
+                scalar1=(1.0, -1.0)[c],
+                scalar2=0.0,
+                op0=MULT,
+                op1=ADD,
+            )
+            f2g[ch] = grouped
+
+        def quantize_f2(ch):
+            c, half = divmod(ch, 2)
+            cols = slice(half * 256, (half + 1) * 256)
+            quantize(f2q[c][:, cols], f2sc[c][:, cols], f2g[ch][:])
+
+        def first_stage(s):
+            b, kt = divmod(s, KT)
+            for c in range(2):
+                bank = psum.tile([P, N], F32, name="abank", tag="a", bufs=4)
+                cols = slice(c * P, (c + 1) * P)
+                nc.tensor.matmul_mx(
+                    out=bank[:],
+                    lhsT=f1q[kt][:, cols].bitcast(FP8X4),
+                    lhsT_scale=f1sc[kt][:, cols],
+                    rhs=xq[b][:].bitcast(FP8X4),
+                    rhs_scale=xsc[b][:],
+                    start=True,
+                    stop=True,
+                )
+                a_banks[(s, c)] = bank
+
+        def products(s, c, parts=((0, 2),)):
+            kt = s % KT
+            g = min(kt, 2)
+            prod = work.tile([P, PACK, 2, P], F32, name="prod%d" % c)
+            for lo, hi in parts:
+                table = tw[g][:, 1 - c + lo : 1 - c + hi, kt - t_groups[g][0], :]
+                a = a_banks[(s, c)][:].rearrange("p (g t r) -> p g t r", t=PACK, r=8)
+                nc.vector.tensor_tensor(
+                    out=prod[:, :, lo:hi, :].rearrange("p t c (g r) -> p c g t r", r=8),
+                    in0=a.unsqueeze(1).to_broadcast([P, hi - lo, 16, PACK, 8]),
+                    in1=table.rearrange("p c (g t r) -> p c g t r", t=PACK, r=8),
+                    op=MULT,
+                )
+            prods[(s, c)] = prod
+
+        def turn(s, c):
+            for d in range(2):
+                if c == 0:
+                    p_banks[(s, d)] = psum.tile([P, PACK, P], F32, name="pbank", tag="p", bufs=2)
+                for t in range(PACK):
+                    nc.tensor.matmul(
+                        out=p_banks[(s, d)][:, t, :],
+                        lhsT=prods[(s, c)][:, t, d, :],
+                        rhs=ident[:],
+                        is_transpose=True,
+                        start=(c == 0 and t == 0),
+                        stop=(c == 1 and t == PACK - 1),
+                    )
+
+        def add_and_turn(s):
+            turn(s, 0)
+            turn(s, 1)
+
+        def copy_p(s, last=False):
+            grouped = work.tile([P, 2, P, PACK], BF16, name="pgrouped", bufs=3, align_bytes=64)
+            for d in range(2):
+                src = p_banks[(s, d)][:].rearrange("p t k -> p k t")
+                if last and d == 1:
+                    nc.vector.tensor_copy(out=grouped[:, d, :, :], in_=src)
+                else:
+                    nc.scalar.copy(out=grouped[:, d, :, :], in_=src)
+            pg[s] = grouped
+
+        def quantize_p(s):
+            quantize(pq[s][:], psc[s][:], pg[s][:].rearrange("p d k t -> p (d k t)"))
+
+        def second_stage(s):
+            bank = psum.tile([P, N], F32, name="obank", tag="o", bufs=2)
+            for d in range(2):
+                cols = slice(d * P, (d + 1) * P)
+                nc.tensor.matmul_mx(
+                    out=bank[:],
+                    lhsT=pq[s][:, cols].bitcast(FP8X4),
+                    lhsT_scale=psc[s][:, cols],
+                    rhs=f2q[d][:].bitcast(FP8X4),
+                    rhs_scale=f2sc[d][:],
+                    start=(d == 0),
+                    stop=(d == 1),
+                )
+            o_banks[s] = bank
+
+        def store(s, on_vector=False):
+            b, kt = divmod(s, KT)
+            result = work.tile([P, N], F32, name="result", bufs=4)
+            if on_vector:
+                nc.vector.tensor_copy(out=result[:], in_=o_banks[s][:])
+            else:
+                nc.scalar.copy(out=result[:], in_=o_banks[s][:])
+            nc.sync.dma_start(out=by_tile(out[b])[:, kt, :], in_=result[:])
+
+        for t in range(3):
+            widen_x(0, t, True)
+        widen_x(0, 3, False)
+        transpose_f1(0)
+        copy_f1(0)
+        interleave_x(0, 0, 384, True)
+        interleave_x(0, 384, 512, False)
+        transpose_f1(1)
+        copy_f1(1)
+        quantize_f1(0)
+        negate_ti(0)
+        quantize_x(0)
+        first_stage(0)
+        quantize_f1(1)
+        first_stage(1)
+        transpose_f1(2)
+        copy_f1(2)
+
+        interleave_f2(0)
+        products(0, 0)
+        products(0, 1)
+        for t in range(PACK):
+            widen_x(1, t, False)
+        interleave_x(1, 0, 256, False)
+        transpose_f1(3)
+        copy_f1(3)
+        add_and_turn(0)
+        negate_ti(1)
+        quantize_f1(2)
+        quantize_f2(0)
+        copy_p(0)
+        first_stage(2)
+        interleave_f2(1)
+        products(1, 0)
+        products(1, 1)
+        interleave_x(1, 256, 512, False)
+        add_and_turn(1)
+        negate_ti(2)
+        quantize_f1(3)
+        quantize_f2(1)
+        copy_p(1)
+        first_stage(3)
+        interleave_f2(2)
+        products(2, 0)
+        products(2, 1)
+        add_and_turn(2)
+        quantize_x(1)
+        quantize_p(0)
+        quantize_f2(2)
+        copy_p(2)
+        first_stage(4)
+        interleave_f2(3)
+        products(3, 0)
+        products(3, 1)
+        add_and_turn(3)
+        quantize_p(1)
+        quantize_p(2)
+        quantize_f2(3)
+        copy_p(3)
+        first_stage(5)
+        second_stage(0)
+        store(0)
+        pending = 1
+        for s in range(4, STEPS - 1):
+            products(s, 0)
+            products(s, 1)
+            add_and_turn(s)
+            quantize_p(s - 1)
+            copy_p(s)
+            if s + 2 < STEPS:
+                first_stage(s + 2)
+                todo = [pending]
+            else:
+                todo = [pending, pending + 1]
+            for o in todo:
+                second_stage(o)
+            for o in todo:
+                store(o)
+            pending = todo[-1] + 1
+        s = STEPS - 1
+        products(s, 0)
+        turn(s, 0)
+        products(s, 1, ((0, 1), (1, 2)))
+        quantize_p(s - 1)
+        turn(s, 1)
+        copy_p(s, True)
+        second_stage(s - 2)
+        second_stage(s - 1)
+        for d in range(2):
+            cols = slice(d * P, (d + 1) * P)
+            quantize(pq[s][:, cols], psc[s][:, cols], pg[s][:, d, :, :].rearrange("p k t -> p (k t)"))
+        store(s - 2)
+        halves = [psum.tile([P, N // 2], F32, name="ohalf", tag="a", bufs=4) for h in range(2)]
+        for h in range(2):
+            mcols = slice(h * 256, (h + 1) * 256)
+            for d in range(2):
+                cols = slice(d * P, (d + 1) * P)
+                nc.tensor.matmul_mx(
+                    out=halves[h][:],
+                    lhsT=pq[s][:, cols].bitcast(FP8X4),
+                    lhsT_scale=psc[s][:, cols],
+                    rhs=f2q[d][:, mcols].bitcast(FP8X4),
+                    rhs_scale=f2sc[d][:, mcols],
+                    start=(d == 0),
+                    stop=(d == 1),
+                )
+        store(s - 1, True)
+        for h in range(2):
+            mcols = slice(h * 256, (h + 1) * 256)
+            part = work.tile([P, N // 2], F32, name="part")
+            if h == 0:
+                nc.scalar.copy(out=part[:], in_=halves[h][:])
+            else:
+                nc.vector.tensor_copy(out=part[:], in_=halves[h][:])
+            nc.sync.dma_start(out=by_tile(out[B - 1])[:, KT - 1, mcols], in_=part[:])

@@ -35,7 +35,7 @@ def tile_learnedfoursteptwiddletransform_kernel(tc, x_bytes, x_scale, f1r, f1i, 
 
         xs = keep.tile([P, PACK], F32, name="xs")
         xb = [keep.tile([P, PACK * N], U8, name="xbytes%d" % b) for b in range(B)]
-        f1_groups = [(0, 1), (1, 3), (3, 4)]
+        f1_groups = [(0, 1), (1, 2), (2, 3), (3, 4)]
         t_groups = [(0, 1), (1, 2), (2, 4)]
         f1_raw = {}
         tw = {}
@@ -71,13 +71,16 @@ def tile_learnedfoursteptwiddletransform_kernel(tc, x_bytes, x_scale, f1r, f1i, 
         load_f1(1)
         load_x(1)
         load_f2(0)
-        load_t(1)
         load_f1(2)
+        load_t(1)
+        load_f1(3)
         load_t(2)
         load_f2(1)
 
         ident = keep.tile([P, P], F32, name="ident")
         make_identity(nc, ident[:])
+        zeros = keep.tile([P, N], BF16, name="zeros")
+        nc.vector.memset(zeros[:], 0.0)
 
         xw = [keep.tile([P, PACK, N], BF16, name="xw%d" % b) for b in range(B)]
         xg = [keep.tile([P, N, PACK], BF16, name="xg%d" % b, align_bytes=64) for b in range(B)]
@@ -127,12 +130,13 @@ def tile_learnedfoursteptwiddletransform_kernel(tc, x_bytes, x_scale, f1r, f1i, 
                     nc.tensor.transpose(bank[:, c, u, :], words[:, u : 2 * P : 2], ident[:])
             f1_banks[kt] = bank
 
-        def copy_f1(kt):
-            if kt == 1:
+        def copy_f1(kt, on_vector=False):
+            if kt == 0:
                 grouped = keep.tile([P, 2 * P * PACK], BF16, name="f1stage", tag="stage", align_bytes=64)
             else:
                 grouped = keep.tile([P, 2 * P * PACK], BF16, name="f1g%d" % kt, align_bytes=64)
-            nc.scalar.copy(
+            move = nc.vector.tensor_copy if on_vector else nc.scalar.copy
+            move(
                 out=grouped[:].bitcast(F32).rearrange("p (c k u) -> p c k u", c=2, u=2),
                 in_=f1_banks[kt][:].rearrange("p c u k -> p c k u"),
             )
@@ -146,17 +150,27 @@ def tile_learnedfoursteptwiddletransform_kernel(tc, x_bytes, x_scale, f1r, f1i, 
                 out=tw[g][:, 0, :, :], in0=tw[g][:, 2, :, :], scalar1=-1.0, scalar2=None, op0=MULT
             )
 
-        def interleave_f2(ch):
+        def interleave_f2(ch, on_scalar=False):
             c, half = divmod(ch, 2)
-            grouped = keep.tile([P, 2 * P * PACK], BF16, name="f2stage", tag="stage", align_bytes=64)
-            nc.gpsimd.tensor_scalar(
-                out=grouped[:].rearrange("p (m t) -> p m t", t=PACK),
-                in0=f2_raw[c][:, :, half * 256 : (half + 1) * 256].rearrange("p t m -> p m t"),
-                scalar1=(1.0, -1.0)[c],
-                scalar2=0.0,
-                op0=MULT,
-                op1=ADD,
-            )
+            src = f2_raw[c][:, :, half * 256 : (half + 1) * 256]
+            if on_scalar:
+                grouped = keep.tile([P, 2 * P * PACK], BF16, name="f2last", align_bytes=64)
+                nc.scalar.activation(
+                    out=grouped[:].rearrange("p (c i t) -> p c t i", i=4, t=PACK),
+                    in_=src.rearrange("p t (c i) -> p c t i", i=4),
+                    func=COPY,
+                    scale=(1.0, -1.0)[c],
+                )
+            else:
+                grouped = keep.tile([P, 2 * P * PACK], BF16, name="f2stage", tag="stage", align_bytes=64)
+                nc.gpsimd.tensor_scalar(
+                    out=grouped[:].rearrange("p (m t) -> p m t", t=PACK),
+                    in0=src.rearrange("p t m -> p m t"),
+                    scalar1=(1.0, -1.0)[c],
+                    scalar2=0.0,
+                    op0=MULT,
+                    op1=ADD,
+                )
             f2g[ch] = grouped
 
         def quantize_f2(ch):
@@ -164,9 +178,9 @@ def tile_learnedfoursteptwiddletransform_kernel(tc, x_bytes, x_scale, f1r, f1i, 
             cols = slice(half * 256, (half + 1) * 256)
             quantize(f2q[c][:, cols], f2sc[c][:, cols], f2g[ch][:])
 
-        def first_stage(s):
+        def first_stage(s, parts=(0, 1)):
             b, kt = divmod(s, KT)
-            for c in range(2):
+            for c in parts:
                 bank = psum.tile([P, N], F32, name="abank", tag="a", bufs=4)
                 cols = slice(c * P, (c + 1) * P)
                 nc.tensor.matmul_mx(
@@ -179,6 +193,11 @@ def tile_learnedfoursteptwiddletransform_kernel(tc, x_bytes, x_scale, f1r, f1i, 
                     stop=True,
                 )
                 a_banks[(s, c)] = bank
+
+        def keep_warm(src, count, tag):
+            bank = psum.tile([P, N], F32, name="warm", tag=tag, bufs=2)
+            for i in range(count):
+                nc.tensor.matmul(out=bank[:], lhsT=src[:, 0:P], rhs=src, start=True, stop=True)
 
         def products(s, c, parts=((0, 2),)):
             kt = s % KT
@@ -195,8 +214,8 @@ def tile_learnedfoursteptwiddletransform_kernel(tc, x_bytes, x_scale, f1r, f1i, 
                 )
             prods[(s, c)] = prod
 
-        def turn(s, c):
-            for d in range(2):
+        def turn(s, c, parts=(0, 1)):
+            for d in parts:
                 if c == 0:
                     p_banks[(s, d)] = psum.tile([P, PACK, P], F32, name="pbank", tag="p", bufs=2)
                 for t in range(PACK):
@@ -209,29 +228,65 @@ def tile_learnedfoursteptwiddletransform_kernel(tc, x_bytes, x_scale, f1r, f1i, 
                         stop=(c == 1 and t == PACK - 1),
                     )
 
-        def add_and_turn(s):
-            turn(s, 0)
-            turn(s, 1)
+        def add_and_turn(s, parts=(0, 1)):
+            turn(s, 0, parts)
+            turn(s, 1, parts)
 
-        def copy_p(s, last=False):
-            grouped = work.tile([P, 2, P, PACK], BF16, name="pgrouped", bufs=3, align_bytes=64)
-            for d in range(2):
+        summed = {}
+
+        def add_pi(s):
+            total = work.tile([P, 2, P, 2], BF16, name="pisum")
+            nc.gpsimd.tensor_tensor(
+                out=total[:],
+                in0=prods[(s, 0)][:, :, 1, :].rearrange("p (u e) q -> p u q e", e=2),
+                in1=prods[(s, 1)][:, :, 1, :].rearrange("p (u e) q -> p u q e", e=2),
+                op=ADD,
+            )
+            summed[s] = total
+
+        def turn_pi(s):
+            bank = psum.tile([P, 2, P], F32, name="pibank", tag="p", bufs=2)
+            words = summed[s][:].rearrange("p u q e -> p (u q e)").bitcast(F32)
+            for u in range(2):
+                nc.tensor.transpose(bank[:, u, :], words[:, u * P : (u + 1) * P], ident[:])
+            p_banks[(s, 1)] = bank
+
+        def copy_p(s, last=False, parts=(0, 1)):
+            if s not in pg:
+                pg[s] = work.tile([P, 2, P, PACK], BF16, name="pgrouped", bufs=3, align_bytes=64)
+            for d in parts:
                 src = p_banks[(s, d)][:].rearrange("p t k -> p k t")
+                dst = pg[s][:, d, :, :]
+                if d == 1 and s in summed:
+                    dst = dst.rearrange("p k t -> p (k t)").bitcast(F32).rearrange("p (k u) -> p k u", u=2)
                 if last and d == 1:
-                    nc.vector.tensor_copy(out=grouped[:, d, :, :], in_=src)
+                    nc.vector.tensor_copy(out=dst, in_=src)
                 else:
-                    nc.scalar.copy(out=grouped[:, d, :, :], in_=src)
-            pg[s] = grouped
+                    nc.scalar.copy(out=dst, in_=src)
+
+        def keep_warm_mx(count):
+            bank = psum.tile([P, N], F32, name="warmmx", tag="o", bufs=2)
+            for i in range(count):
+                nc.tensor.matmul_mx(
+                    out=bank[:],
+                    lhsT=f1q[0][:, 0:P].bitcast(FP8X4),
+                    lhsT_scale=f1sc[0][:, 0:P],
+                    rhs=xq[0][:].bitcast(FP8X4),
+                    rhs_scale=xsc[0][:],
+                    start=True,
+                    stop=True,
+                )
 
         def quantize_p(s):
             quantize(pq[s][:], psc[s][:], pg[s][:].rearrange("p d k t -> p (d k t)"))
 
-        def second_stage(s):
-            bank = psum.tile([P, N], F32, name="obank", tag="o", bufs=2)
-            for d in range(2):
+        def second_stage(s, parts=(0, 1)):
+            for d in parts:
+                if d == 0:
+                    o_banks[s] = psum.tile([P, N], F32, name="obank", tag="o", bufs=2)
                 cols = slice(d * P, (d + 1) * P)
                 nc.tensor.matmul_mx(
-                    out=bank[:],
+                    out=o_banks[s][:],
                     lhsT=pq[s][:, cols].bitcast(FP8X4),
                     lhsT_scale=psc[s][:, cols],
                     rhs=f2q[d][:].bitcast(FP8X4),
@@ -239,7 +294,6 @@ def tile_learnedfoursteptwiddletransform_kernel(tc, x_bytes, x_scale, f1r, f1i, 
                     start=(d == 0),
                     stop=(d == 1),
                 )
-            o_banks[s] = bank
 
         def store(s, on_vector=False):
             b, kt = divmod(s, KT)
@@ -250,118 +304,144 @@ def tile_learnedfoursteptwiddletransform_kernel(tc, x_bytes, x_scale, f1r, f1i, 
                 nc.scalar.copy(out=result[:], in_=o_banks[s][:])
             nc.sync.dma_start(out=by_tile(out[b])[:, kt, :], in_=result[:])
 
-        for t in range(3):
-            widen_x(0, t, True)
+        def finish():
+            s = STEPS - 1
+            for d in range(2):
+                cols = slice(d * P, (d + 1) * P)
+                quantize(pq[s][:, cols], psc[s][:, cols], pg[s][:, d, :, :].rearrange("p k t -> p (k t)"))
+            store(s - 1)
+            halves = [psum.tile([P, N // 2], F32, name="ohalf", tag="a", bufs=4) for h in range(2)]
+            for h in range(2):
+                mcols = slice(h * 256, (h + 1) * 256)
+                for d in range(2):
+                    cols = slice(d * P, (d + 1) * P)
+                    nc.tensor.matmul_mx(
+                        out=halves[h][:],
+                        lhsT=pq[s][:, cols].bitcast(FP8X4),
+                        lhsT_scale=psc[s][:, cols],
+                        rhs=f2q[d][:, mcols].bitcast(FP8X4),
+                        rhs_scale=f2sc[d][:, mcols],
+                        start=(d == 0),
+                        stop=(d == 1),
+                    )
+            for h in range(2):
+                mcols = slice(h * 256, (h + 1) * 256)
+                part = work.tile([P, N // 2], F32, name="part")
+                if h == 0:
+                    nc.scalar.copy(out=part[:], in_=halves[h][:])
+                else:
+                    nc.vector.tensor_copy(out=part[:], in_=halves[h][:])
+                nc.sync.dma_start(out=by_tile(out[B - 1])[:, KT - 1, mcols], in_=part[:])
+
+
+        keep_warm(zeros[:], 4, "p")
+        widen_x(0, 0, True)
+        widen_x(0, 1, True)
+        widen_x(0, 2, True)
         widen_x(0, 3, False)
         transpose_f1(0)
-        copy_f1(0)
         interleave_x(0, 0, 384, True)
         interleave_x(0, 384, 512, False)
+        copy_f1(0)
+        keep_warm(zeros[:], 2, "p")
         transpose_f1(1)
-        copy_f1(1)
-        quantize_f1(0)
+        keep_warm(zeros[:], 2, "p")
         negate_ti(0)
         quantize_x(0)
+        quantize_f1(0)
         first_stage(0)
-        quantize_f1(1)
-        first_stage(1)
+        copy_f1(1, True)
+        widen_x(1, 0, False)
+        widen_x(1, 1, False)
+        widen_x(1, 2, False)
+        widen_x(1, 3, False)
+        interleave_x(1, 0, 256, False)
         transpose_f1(2)
         copy_f1(2)
 
         interleave_f2(0)
         products(0, 0)
+        turn(0, 0)
+        keep_warm(zeros[:], 2, "o")
         products(0, 1)
-        for t in range(PACK):
-            widen_x(1, t, False)
-        interleave_x(1, 0, 256, False)
-        transpose_f1(3)
-        copy_f1(3)
-        add_and_turn(0)
+        quantize_f1(1)
+        first_stage(1)
+        turn(0, 1)
         negate_ti(1)
         quantize_f1(2)
         quantize_f2(0)
-        copy_p(0)
         first_stage(2)
+        transpose_f1(3)
+        interleave_x(1, 256, 512, False)
+        copy_p(0)
+        copy_f1(3)
+
         interleave_f2(1)
         products(1, 0)
+        turn(1, 0)
+        keep_warm(zeros[:], 1, "o")
         products(1, 1)
-        interleave_x(1, 256, 512, False)
-        add_and_turn(1)
+        turn(1, 1)
         negate_ti(2)
+        quantize_x(1)
         quantize_f1(3)
         quantize_f2(1)
-        copy_p(1)
         first_stage(3)
+        interleave_f2(3, True)
+        copy_p(1)
+
         interleave_f2(2)
         products(2, 0)
+        turn(2, 0)
+        keep_warm(zeros[:], 1, "o")
         products(2, 1)
-        add_and_turn(2)
-        quantize_x(1)
+        turn(2, 1)
         quantize_p(0)
+        quantize_f2(3)
+        quantize_p(1)
         quantize_f2(2)
-        copy_p(2)
         first_stage(4)
-        interleave_f2(3)
+        second_stage(0)
+        second_stage(1)
+        copy_p(2)
+        store(0)
+        store(1)
         products(3, 0)
         products(3, 1)
         add_and_turn(3)
-        quantize_p(1)
         quantize_p(2)
-        quantize_f2(3)
-        copy_p(3)
         first_stage(5)
-        second_stage(0)
-        store(0)
-        pending = 1
-        for s in range(4, STEPS - 1):
-            products(s, 0)
-            products(s, 1)
-            add_and_turn(s)
-            quantize_p(s - 1)
-            copy_p(s)
-            if s + 2 < STEPS:
-                first_stage(s + 2)
-                todo = [pending]
-            else:
-                todo = [pending, pending + 1]
-            for o in todo:
-                second_stage(o)
-            for o in todo:
-                store(o)
-            pending = todo[-1] + 1
-        s = STEPS - 1
-        products(s, 0)
-        turn(s, 0)
-        products(s, 1, ((0, 1), (1, 2)))
-        quantize_p(s - 1)
-        turn(s, 1)
-        copy_p(s, True)
-        second_stage(s - 2)
-        second_stage(s - 1)
-        for d in range(2):
-            cols = slice(d * P, (d + 1) * P)
-            quantize(pq[s][:, cols], psc[s][:, cols], pg[s][:, d, :, :].rearrange("p k t -> p (k t)"))
-        store(s - 2)
-        halves = [psum.tile([P, N // 2], F32, name="ohalf", tag="a", bufs=4) for h in range(2)]
-        for h in range(2):
-            mcols = slice(h * 256, (h + 1) * 256)
-            for d in range(2):
-                cols = slice(d * P, (d + 1) * P)
-                nc.tensor.matmul_mx(
-                    out=halves[h][:],
-                    lhsT=pq[s][:, cols].bitcast(FP8X4),
-                    lhsT_scale=psc[s][:, cols],
-                    rhs=f2q[d][:, mcols].bitcast(FP8X4),
-                    rhs_scale=f2sc[d][:, mcols],
-                    start=(d == 0),
-                    stop=(d == 1),
-                )
-        store(s - 1, True)
-        for h in range(2):
-            mcols = slice(h * 256, (h + 1) * 256)
-            part = work.tile([P, N // 2], F32, name="part")
-            if h == 0:
-                nc.scalar.copy(out=part[:], in_=halves[h][:])
-            else:
-                nc.vector.tensor_copy(out=part[:], in_=halves[h][:])
-            nc.sync.dma_start(out=by_tile(out[B - 1])[:, KT - 1, mcols], in_=part[:])
+        second_stage(2)
+        copy_p(3)
+        store(2)
+        products(4, 0)
+        products(4, 1)
+        add_and_turn(4)
+        quantize_p(3)
+        first_stage(6)
+        second_stage(3)
+        copy_p(4)
+        store(3)
+        products(5, 0)
+        products(5, 1)
+        add_and_turn(5)
+        quantize_p(4)
+        first_stage(7)
+        second_stage(4)
+        copy_p(5)
+        store(4)
+        products(6, 0)
+        products(6, 1)
+        add_and_turn(6)
+        quantize_p(5)
+        second_stage(5)
+        copy_p(6)
+        store(5)
+        products(7, 0)
+        turn(7, 0)
+        products(7, 1, ((0, 1), (1, 2)))
+        quantize_p(6)
+        turn(7, 1)
+        copy_p(7, True)
+        second_stage(6)
+        finish()

from contextlib import ExitStack

import concourse.mybir as mybir
from concourse.masks import make_identity

F32 = mybir.dt.float32
BF16 = mybir.dt.bfloat16
U32 = mybir.dt.uint32
U8 = mybir.dt.uint8
FP8 = mybir.dt.float8_e4m3fn
FP8X4 = mybir.dt.float8_e4m3fn_x4
MULT = mybir.AluOpType.mult
ADD = mybir.AluOpType.add
COPY = mybir.ActivationFunctionType.Copy

P = 128
PACK = 4
N = 512
B = 2
KT = 4
STEPS = B * KT
FLOPS = 2 * 4 * 2 * 512 * 512 * 512


def tile_learnedfoursteptwiddletransform_kernel(tc, x_bytes, x_scale, f1r, f1i, tr, ti, f2r, f2i, out):
    nc = tc.nc
    with ExitStack() as ctx:
        keep = ctx.enter_context(tc.tile_pool(name="keep", bufs=1))
        work = ctx.enter_context(tc.tile_pool(name="work", bufs=2))
        psum = ctx.enter_context(tc.psum_pool(name="psum", bufs=1))
        ctx.enter_context(tc.manual_schedule())

        def by_tile(mat):
            return mat.rearrange("(p a) j -> p a j", a=KT)

        xs = keep.tile([P, PACK], F32, name="xs")
        xb = [keep.tile([P, PACK * N], U8, name="xbytes%d" % b) for b in range(B)]
        f1_groups = [(0, 1), (1, 2), (2, 3), (3, 4)]
        t_groups = [(0, 1), (1, 2), (2, 4)]
        f1_raw = {}
        tw = {}
        f2_raw = [keep.tile([P, PACK, N], BF16, name="f2raw%d" % c) for c in range(2)]

        def load_x(b):
            nc.sync.dma_start(out=xb[b][:], in_=x_bytes[b].rearrange("(p t) n -> p (t n)", t=PACK))

        def load_f1(g):
            lo, hi = f1_groups[g]
            for c, mat in enumerate((f1r, f1i)):
                raw = keep.tile([P, hi - lo, N], BF16, name="f1raw%d_%d" % (g, c))
                nc.sync.dma_start(out=raw[:], in_=by_tile(mat)[:, lo:hi, :])
                for kt in range(lo, hi):
                    f1_raw[(kt, c)] = raw[:, kt - lo, :]

        def load_t(g):
            lo, hi = t_groups[g]
            table = keep.tile([P, 3, hi - lo, N], BF16, name="tw%d" % g)
            for slot, mat in ((1, tr), (2, ti)):
                nc.sync.dma_start(out=table[:, slot, :, :], in_=by_tile(mat)[:, lo:hi, :])
            tw[g] = table

        def load_f2(c):
            rows = (f2r, f2i)[c].rearrange("(g t r) m -> t g r m", t=PACK, r=8)
            for t in range(PACK):
                nc.sync.dma_start(out=f2_raw[c][:, t, :], in_=rows[t])

        nc.sync.dma_start(out=xs[:], in_=x_scale.rearrange("o (p t) z -> p (o t z)", t=PACK))
        load_x(0)
        load_f1(0)
        load_t(0)
        load_f1(1)
        load_x(1)
        load_f2(0)
        load_f1(2)
        load_t(1)
        load_f1(3)
        load_t(2)
        load_f2(1)

        ident = keep.tile([P, P], F32, name="ident")
        make_identity(nc, ident[:])
        zeros = keep.tile([P, N], BF16, name="zeros")
        nc.vector.memset(zeros[:], 0.0)

        xw = [keep.tile([P, PACK, N], BF16, name="xw%d" % b) for b in range(B)]
        xg = [keep.tile([P, N, PACK], BF16, name="xg%d" % b, align_bytes=64) for b in range(B)]
        xq = [keep.tile([P, N], U32, name="xq%d" % b, align_bytes=64) for b in range(B)]
        xsc = [keep.tile([P, N], U8, name="xsc%d" % b, align_bytes=64) for b in range(B)]
        f1g = {}
        f1q = [keep.tile([P, 2 * P], U32, name="f1q%d" % kt, align_bytes=64) for kt in range(KT)]
        f1sc = [keep.tile([P, 2 * P], U8, name="f1sc%d" % kt, align_bytes=64) for kt in range(KT)]
        f2q = [keep.tile([P, N], U32, name="f2q%d" % c, align_bytes=64) for c in range(2)]
        f2sc = [keep.tile([P, N], U8, name="f2sc%d" % c, align_bytes=64) for c in range(2)]
        pq = [keep.tile([P, 2 * P], U32, name="pq%d" % s, align_bytes=64) for s in range(STEPS)]
        psc = [keep.tile([P, 2 * P], U8, name="psc%d" % s, align_bytes=64) for s in range(STEPS)]
        a_banks = {}
        prods = {}
        p_banks = {}
        pg = {}
        f1_banks = {}
        o_banks = {}
        f2g = {}

        def quantize(codes, scales, src):
            nc.vector.quantize_mx(out=codes.bitcast(FP8X4), scales=scales, in_=src)

        def widen_x(b, t, on_vector):
            src = xb[b][:, t * N : (t + 1) * N].bitcast(FP8)
            if on_vector:
                nc.vector.tensor_scalar(out=xw[b][:, t, :], in0=src, scalar1=xs[:, t : t + 1], scalar2=None, op0=MULT)
            else:
                nc.scalar.activation(out=xw[b][:, t, :], in_=src, func=COPY, scale=xs[:, t : t + 1])

        def interleave_x(b, lo, hi, on_vector):
            dst = xg[b][:, lo:hi, :].rearrange("p (c i) t -> p c t i", i=4)
            src = xw[b][:, :, lo:hi].rearrange("p t (c i) -> p c t i", i=4)
            if on_vector:
                nc.vector.tensor_copy(out=dst, in_=src)
            else:
                nc.scalar.copy(out=dst, in_=src)

        def quantize_x(b):
            quantize(xq[b][:], xsc[b][:], xg[b][:].rearrange("p n t -> p (n t)"))

        def transpose_f1(kt):
            bank = psum.tile([P, 2, 2, P], F32, name="f1bank", tag="o", bufs=2)
            for c in range(2):
                words = f1_raw[(kt, c)].bitcast(F32)
                for u in range(2):
                    nc.tensor.transpose(bank[:, c, u, :], words[:, u : 2 * P : 2], ident[:])
            f1_banks[kt] = bank

        def copy_f1(kt, on_vector=False):
            if kt == 0:
                grouped = keep.tile([P, 2 * P * PACK], BF16, name="f1stage", tag="stage", align_bytes=64)
            else:
                grouped = keep.tile([P, 2 * P * PACK], BF16, name="f1g%d" % kt, align_bytes=64)
            move = nc.vector.tensor_copy if on_vector else nc.scalar.copy
            move(
                out=grouped[:].bitcast(F32).rearrange("p (c k u) -> p c k u", c=2, u=2),
                in_=f1_banks[kt][:].rearrange("p c u k -> p c k u"),
            )
            f1g[kt] = grouped

        def quantize_f1(kt):
            quantize(f1q[kt][:], f1sc[kt][:], f1g[kt][:])

        def negate_ti(g):
            nc.vector.tensor_scalar(
                out=tw[g][:, 0, :, :], in0=tw[g][:, 2, :, :], scalar1=-1.0, scalar2=None, op0=MULT
            )

        def interleave_f2(ch, on_scalar=False):
            c, half = divmod(ch, 2)
            src = f2_raw[c][:, :, half * 256 : (half + 1) * 256]
            if on_scalar:
                grouped = keep.tile([P, 2 * P * PACK], BF16, name="f2last", align_bytes=64)
                nc.scalar.activation(
                    out=grouped[:].rearrange("p (c i t) -> p c t i", i=4, t=PACK),
                    in_=src.rearrange("p t (c i) -> p c t i", i=4),
                    func=COPY,
                    scale=(1.0, -1.0)[c],
                )
            else:
                grouped = keep.tile([P, 2 * P * PACK], BF16, name="f2stage", tag="stage", align_bytes=64)
                nc.gpsimd.tensor_scalar(
                    out=grouped[:].rearrange("p (m t) -> p m t", t=PACK),
                    in0=src.rearrange("p t m -> p m t"),
                    scalar1=(1.0, -1.0)[c],
                    scalar2=0.0,
                    op0=MULT,
                    op1=ADD,
                )
            f2g[ch] = grouped

        def quantize_f2(ch):
            c, half = divmod(ch, 2)
            cols = slice(half * 256, (half + 1) * 256)
            quantize(f2q[c][:, cols], f2sc[c][:, cols], f2g[ch][:])

        def first_stage(s, parts=(0, 1)):
            b, kt = divmod(s, KT)
            for c in parts:
                bank = psum.tile([P, N], F32, name="abank", tag="a", bufs=4)
                cols = slice(c * P, (c + 1) * P)
                nc.tensor.matmul_mx(
                    out=bank[:],
                    lhsT=f1q[kt][:, cols].bitcast(FP8X4),
                    lhsT_scale=f1sc[kt][:, cols],
                    rhs=xq[b][:].bitcast(FP8X4),
                    rhs_scale=xsc[b][:],
                    start=True,
                    stop=True,
                )
                a_banks[(s, c)] = bank

        def keep_warm(src, count, tag):
            bank = psum.tile([P, N], F32, name="warm", tag=tag, bufs=2)
            for i in range(count):
                nc.tensor.matmul(out=bank[:], lhsT=src[:, 0:P], rhs=src, start=True, stop=True)

        def products(s, c, parts=((0, 2),)):
            kt = s % KT
            g = min(kt, 2)
            prod = work.tile([P, PACK, 2, P], F32, name="prod%d" % c)
            for lo, hi in parts:
                table = tw[g][:, 1 - c + lo : 1 - c + hi, kt - t_groups[g][0], :]
                a = a_banks[(s, c)][:].rearrange("p (g t r) -> p g t r", t=PACK, r=8)
                nc.vector.tensor_tensor(
                    out=prod[:, :, lo:hi, :].rearrange("p t c (g r) -> p c g t r", r=8),
                    in0=a.unsqueeze(1).to_broadcast([P, hi - lo, 16, PACK, 8]),
                    in1=table.rearrange("p c (g t r) -> p c g t r", t=PACK, r=8),
                    op=MULT,
                )
            prods[(s, c)] = prod

        def turn(s, c, parts=(0, 1)):
            for d in parts:
                if c == 0:
                    p_banks[(s, d)] = psum.tile([P, PACK, P], F32, name="pbank", tag="p", bufs=2)
                for t in range(PACK):
                    nc.tensor.matmul(
                        out=p_banks[(s, d)][:, t, :],
                        lhsT=prods[(s, c)][:, t, d, :],
                        rhs=ident[:],
                        is_transpose=True,
                        start=(c == 0 and t == 0),
                        stop=(c == 1 and t == PACK - 1),
                    )

        def add_and_turn(s, parts=(0, 1)):
            turn(s, 0, parts)
            turn(s, 1, parts)

        summed = {}

        def add_pi(s):
            total = work.tile([P, 2, P, 2], BF16, name="pisum")
            nc.gpsimd.tensor_tensor(
                out=total[:],
                in0=prods[(s, 0)][:, :, 1, :].rearrange("p (u e) q -> p u q e", e=2),
                in1=prods[(s, 1)][:, :, 1, :].rearrange("p (u e) q -> p u q e", e=2),
                op=ADD,
            )
            summed[s] = total

        def turn_pi(s):
            bank = psum.tile([P, 2, P], F32, name="pibank", tag="p", bufs=2)
            words = summed[s][:].rearrange("p u q e -> p (u q e)").bitcast(F32)
            for u in range(2):
                nc.tensor.transpose(bank[:, u, :], words[:, u * P : (u + 1) * P], ident[:])
            p_banks[(s, 1)] = bank

        def copy_p(s, last=False, parts=(0, 1)):
            if s not in pg:
                pg[s] = work.tile([P, 2, P, PACK], BF16, name="pgrouped", bufs=3, align_bytes=64)
            for d in parts:
                src = p_banks[(s, d)][:].rearrange("p t k -> p k t")
                dst = pg[s][:, d, :, :]
                if d == 1 and s in summed:
                    dst = dst.rearrange("p k t -> p (k t)").bitcast(F32).rearrange("p (k u) -> p k u", u=2)
                if last and d == 1:
                    nc.vector.tensor_copy(out=dst, in_=src)
                else:
                    nc.scalar.copy(out=dst, in_=src)

        def keep_warm_mx(count):
            bank = psum.tile([P, N], F32, name="warmmx", tag="o", bufs=2)
            for i in range(count):
                nc.tensor.matmul_mx(
                    out=bank[:],
                    lhsT=f1q[0][:, 0:P].bitcast(FP8X4),
                    lhsT_scale=f1sc[0][:, 0:P],
                    rhs=xq[0][:].bitcast(FP8X4),
                    rhs_scale=xsc[0][:],
                    start=True,
                    stop=True,
                )

        def quantize_p(s):
            quantize(pq[s][:], psc[s][:], pg[s][:].rearrange("p d k t -> p (d k t)"))

        def second_stage(s, parts=(0, 1)):
            for d in parts:
                if d == 0:
                    o_banks[s] = psum.tile([P, N], F32, name="obank", tag="o", bufs=2)
                cols = slice(d * P, (d + 1) * P)
                nc.tensor.matmul_mx(
                    out=o_banks[s][:],
                    lhsT=pq[s][:, cols].bitcast(FP8X4),
                    lhsT_scale=psc[s][:, cols],
                    rhs=f2q[d][:].bitcast(FP8X4),
                    rhs_scale=f2sc[d][:],
                    start=(d == 0),
                    stop=(d == 1),
                )

        def store(s, on_vector=False):
            b, kt = divmod(s, KT)
            result = work.tile([P, N], F32, name="result", bufs=4)
            if on_vector:
                nc.vector.tensor_copy(out=result[:], in_=o_banks[s][:])
            else:
                nc.scalar.copy(out=result[:], in_=o_banks[s][:])
            nc.sync.dma_start(out=by_tile(out[b])[:, kt, :], in_=result[:])

        def finish():
            s = STEPS - 1
            for d in range(2):
                cols = slice(d * P, (d + 1) * P)
                quantize(pq[s][:, cols], psc[s][:, cols], pg[s][:, d, :, :].rearrange("p k t -> p (k t)"))
            store(s - 1)
            halves = [psum.tile([P, N // 2], F32, name="ohalf", tag="a", bufs=4) for h in range(2)]
            for h in range(2):
                mcols = slice(h * 256, (h + 1) * 256)
                for d in range(2):
                    cols = slice(d * P, (d + 1) * P)
                    nc.tensor.matmul_mx(
                        out=halves[h][:],
                        lhsT=pq[s][:, cols].bitcast(FP8X4),
                        lhsT_scale=psc[s][:, cols],
                        rhs=f2q[d][:, mcols].bitcast(FP8X4),
                        rhs_scale=f2sc[d][:, mcols],
                        start=(d == 0),
                        stop=(d == 1),
                    )
            for h in range(2):
                mcols = slice(h * 256, (h + 1) * 256)
                part = work.tile([P, N // 2], F32, name="part")
                if h == 0:
                    nc.scalar.copy(out=part[:], in_=halves[h][:])
                else:
                    nc.vector.tensor_copy(out=part[:], in_=halves[h][:])
                nc.sync.dma_start(out=by_tile(out[B - 1])[:, KT - 1, mcols], in_=part[:])


        keep_warm(zeros[:], 4, "p")
        widen_x(0, 0, True)
        widen_x(0, 1, True)
        widen_x(0, 2, True)
        widen_x(0, 3, False)
        transpose_f1(0)
        interleave_x(0, 0, 384, True)
        interleave_x(0, 384, 512, False)
        copy_f1(0)
        keep_warm(zeros[:], 2, "p")
        transpose_f1(1)
        keep_warm(zeros[:], 2, "p")
        negate_ti(0)
        quantize_x(0)
        quantize_f1(0)
        first_stage(0)
        copy_f1(1, True)
        widen_x(1, 0, False)
        widen_x(1, 1, False)
        widen_x(1, 2, False)
        widen_x(1, 3, False)
        interleave_x(1, 0, 256, False)
        transpose_f1(2)
        copy_f1(2)

        interleave_f2(0)
        products(0, 0)
        turn(0, 0)
        keep_warm(zeros[:], 2, "o")
        products(0, 1)
        quantize_f1(1)
        first_stage(1)
        turn(0, 1)
        negate_ti(1)
        quantize_f1(2)
        quantize_f2(0)
        first_stage(2)
        transpose_f1(3)
        interleave_x(1, 256, 512, False)
        copy_p(0)
        copy_f1(3)

        interleave_f2(1)
        products(1, 0)
        turn(1, 0)
        keep_warm(zeros[:], 1, "o")
        products(1, 1)
        turn(1, 1)
        negate_ti(2)
        quantize_x(1)
        quantize_f1(3)
        quantize_f2(1)
        first_stage(3)
        interleave_f2(3, True)
        copy_p(1)

        interleave_f2(2)
        products(2, 0)
        turn(2, 0)
        keep_warm(zeros[:], 1, "o")
        products(2, 1)
        turn(2, 1)
        quantize_p(0)
        quantize_f2(3)
        quantize_p(1)
        quantize_f2(2)
        first_stage(4)
        second_stage(0)
        second_stage(1)
        copy_p(2)
        store(0)
        store(1)
        products(3, 0)
        products(3, 1)
        add_and_turn(3)
        quantize_p(2)
        first_stage(5)
        second_stage(2)
        copy_p(3)
        store(2)
        products(4, 0)
        products(4, 1)
        add_and_turn(4)
        quantize_p(3)
        first_stage(6)
        second_stage(3)
        copy_p(4)
        store(3)
        products(5, 0)
        products(5, 1)
        add_and_turn(5)
        quantize_p(4)
        first_stage(7)
        second_stage(4)
        copy_p(5)
        store(4)
        products(6, 0)
        products(6, 1)
        add_and_turn(6)
        quantize_p(5)
        second_stage(5)
        copy_p(6)
        store(5)
        products(7, 0)
        turn(7, 0)
        products(7, 1, ((0, 1), (1, 2)))
        quantize_p(6)
        turn(7, 1)
        copy_p(7, True)
        second_stage(6)
        finish()
